import numpy as np, ml_dtypes
CORES = [2,6,10,14,18,22,26,30]
N = 8
import mx_ref
BF = ml_dtypes.bfloat16
def entries(a):
    return np.ascontiguousarray(a.T).reshape(-1)
def table(e):
    return np.ascontiguousarray(np.reshape(e, (-1, 16)).T).astype(np.int32)
def gcols(t, e):
    v = np.concatenate([t.reshape(8, 16, -1, 4), np.zeros((8, 16, 1, 4), BF)], axis=2)
    return np.ascontiguousarray(np.stack([v[g][:, e[g]] for g in range(8)])).reshape(128, -1)
def cut(t, i, w=512):
    return t[:, w * i:w * i + w]
def f(rng, *shape):
    return mx_ref.flush((rng.standard_normal(shape, dtype=np.float32) * np.exp2(rng.integers(-2, 3, shape[:-1] + (1,)))).astype(BF))
def wide(rng, *shape, cols=0):
    v = rng.standard_normal(shape, dtype=np.float32) * np.exp2(rng.integers(-12, 13, shape)).astype(np.float32)
    if cols: v *= np.repeat(np.exp2(rng.integers(-cols, cols + 1, shape[:-2] + (1, shape[-1] // 4))) * (rng.random(shape[:-2] + (1, shape[-1] // 4)) > 0.0625), 4, axis=-1).astype(np.float32)
    return mx_ref.flush(v.astype(BF))
K, T, O = 256, 256, 4
SH = (7, 6, 5, 4, 3, 2, 1, 0)
A = (1531, 797, 1877, 1129, 619, 1993, 1367, 911)
B = (1013, 1741, 587, 1459, 1907, 733, 1229, 1667)
def levels(q):
    return list(range(8 // N * q, 8 // N * (q + 1)))
def owned(t):
    t = t.reshape(N, 8, 16, -1).copy()
    for q in range(N):
        for g in range(8):
            if g not in levels(q): t[q, g] = 0
    return t.reshape(N, 128, -1)
def pack(p):
    return np.stack([table(p[r]) for r in range(N)])
def places(rng):
    return {"px": pack(rng.integers(0, 1024, (N, T))), "py": pack(rng.integers(0, 1024, (N, T)))}
def setup_inputs(rng):
    return {"tb": owned(f(rng, N, 128, 4 * K)), **places(rng), "w": f(rng, N, 128, 512 * O)}
def setup_inputs_same(rng):
    d = setup_inputs(rng)
    d["px"] = pack(np.repeat(rng.integers(0, 1024, (N, 1)), T, axis=1)); d["py"] = pack(np.repeat(rng.integers(0, 1024, (N, 1)), T, axis=1))
    return d
def setup_inputs_corner(rng):
    d = setup_inputs(rng); c = rng.integers(0, 4, (N, T))
    for r in range(N): c[r, rng.permutation(T)[:4]] = np.arange(4)
    d["px"] = pack((c & 1) * 1023); d["py"] = pack((c >> 1) * 1023)
    return d
def setup_inputs_alike(rng):
    d = setup_inputs(rng)
    d["px"] = pack(np.repeat(rng.integers(0, 1024, (1, T)), N, axis=0)); d["py"] = pack(np.repeat(rng.integers(0, 1024, (1, T)), N, axis=0))
    return d
def setup_inputs_line(rng):
    d = setup_inputs(rng)
    d["px"] = pack(rng.integers(0, 1025 - T, (N, 1)) + np.arange(T)); d["py"] = pack(np.repeat(rng.integers(0, 1024, (N, 1)), T, axis=1))
    return d
def setup_inputs_spread(rng):
    d = setup_inputs(rng); d["tb"] = owned(wide(rng, N, 128, 4 * K, cols=4)); return d
def check_inputs(d):
    b = []
    for r in range(N):
        for n in ("px", "py"):
            e = entries(d[n][r])
            if e.min() < 0 or e.max() > 1023: b.append(n)
        t = d["tb"][r].reshape(8, 16, -1).astype(np.float32)
        if any((t[g] != 0).any() for g in range(8) if g not in levels(r)): b.append("tb")
    return b
def addresses(x, y):
    return np.stack([((x >> SH[g]) * A[g] + (y >> SH[g]) * B[g]) & (K - 1) for g in range(8)])
def reference(tb, px, py, w):
    y = np.zeros((N, 128, O * T), np.float32)
    for r in range(N):
        e = addresses(entries(px[r]), entries(py[r])); E = []
        for q in range(N):
            a = np.full((8, T), -1); a[levels(q)] = e[levels(q)]
            E.append(mx_ref.quantize(np.ascontiguousarray(gcols(tb[q], a))))
        for o in range(O):
            W = mx_ref.quantize(np.ascontiguousarray(cut(w[r], o)))
            Z = mx_ref.matmul(W, E[0])
            for q in range(1, N): Z = Z + mx_ref.matmul(W, E[q])
            y[r][:, T * o:T * o + T] = Z
    return {"y": y}

@@ -1,0 +1,319 @@
+from concourse.bass import DstId, RemoteDMATransfer
+from concourse.mybir import dt, AluOpType, ActivationFunctionType
+
+SH = (7, 6, 5, 4, 3, 2, 1, 0)
+A = (1531, 797, 1877, 1129, 619, 1993, 1367, 911)
+B = (1013, 1741, 587, 1459, 1907, 733, 1229, 1667)
+BF, F32, I32, U16, X4, U8 = "bfloat16", "float32", "int32", "uint16", "float8_e4m3fn_x4", "uint8"
+
+SCRATCH = {
+    "ct": ("sbuf", [128, 512], BF),
+    "st": ("sbuf", [128, 1024], BF),
+    "wn": ("sbuf", [128, 1024], BF),
+    "zt": ("sbuf", [128, 512], BF),
+    "sn0": ("sbuf", [128, 2048], BF), "sn1": ("sbuf", [128, 2048], BF),
+    "sf0": ("sbuf", [128, 2048], BF), "sf1": ("sbuf", [128, 2048], BF),
+    "xy": ("sbuf", [128, 32], I32),
+    "pi": ("sbuf", [128, 1], I32), "gi": ("sbuf", [128, 1], I32),
+    "kt": ("sbuf", [128, 16], F32), "ka": ("sbuf", [128, 8], F32), "kc": ("sbuf", [128, 4], F32),
+    "un": ("sbuf", [128, 16], I32), "mn": ("sbuf", [128, 16], I32), "an": ("sbuf", [128, 8], I32),
+    "bn": ("sbuf", [128, 8], I32), "offn": ("sbuf", [128, 8], U16),
+    "uf": ("sbuf", [128, 128], I32), "mf": ("sbuf", [128, 128], I32), "sf": ("sbuf", [128, 64], I32),
+    "af": ("sbuf", [128, 64], I32), "hf": ("sbuf", [128, 64], I32), "bf": ("sbuf", [128, 64], I32),
+    "offf": ("sbuf", [128, 128], U16),
+    "arr": ("sbuf", [128, 32], U16),
+    "cq": ("sbuf", [128, 128], X4), "cs": ("sbuf", [128, 128], U8),
+    "eq": ("sbuf", [128, 512], X4), "es": ("sbuf", [128, 512], U8),
+    "farq": ("sbuf", [128, 512], X4), "fars": ("sbuf", [128, 512], U8),
+    "nearq": ("sbuf", [128, 512], X4), "nears": ("sbuf", [128, 512], U8),
+    "pw0": ("sbuf", [128, 2048], F32), "pw1": ("sbuf", [128, 2048], F32),
+    "acc": ("sbuf", [128, 1024], F32), "yo": ("sbuf", [128, 1024], F32),
+    "ps": ("psum", [128, 4096], F32),
+}
+for _n in ("sn0", "sn1", "sf0", "sf1"):
+    SCRATCH[_n + "q"] = ("sbuf", [128, 512], X4)
+    SCRATCH[_n + "s"] = ("sbuf", [128, 512], U8)
+for _s in range(4):
+    SCRATCH["e%d" % _s] = ("sbuf", [128, 512], BF)
+
+SEMAPHORES = ["v", "io_", "ct", "xy", "st", "wn", "wf", "zt", "zf", "tq", "on", "sp", "sn", "sf", "lo", "far0", "far1", "yd"]
+SEMAPHORES += ["%s%d" % (n, s) for n in ("a", "n", "gs", "gv", "eq") for s in range(4)]
+SEMAPHORES += ["%s%d%d%d" % (n, e, oo, b) for n in ("p", "k") for e in range(2) for oo in range(2) for b in range(4)]
+SEMAPHORES += ["f%d%d" % (oo, b) for oo in range(2) for b in range(4)] + ["y0", "y1"]
+
+
+def rank_program(g, core, T, topo):
+    r = T.rank_of(core)
+    if r is None:
+        return
+    S = T.sem
+    cores = list(T.cores)
+    Q, F, slot = r // 4, 1 - r // 4, r % 4
+    copy = ActivationFunctionType.Copy
+    add, sub, mult = AluOpType.add, AluOpType.subtract, AluOpType.mult
+    shr, band = AluOpType.arith_shift_right, AluOpType.bitwise_and
+
+    def chip(q):
+        return topo.chip(cores[q])
+
+    def dst(q):
+        rid, pid, _ = topo.addr(cores[q])
+        return DstId(rid=rid, pnc=pid)
+
+    def bits(es):
+        return sum(1 << e for e in es)
+
+    same_chip = [q for q in range(8) if chip(q) == chip(r)]
+    idx = same_chip.index(r)
+    partner = [q for q in same_chip if q != r][0]
+    mates = [q for q in range(4 * Q, 4 * Q + 4) if q not in same_chip]
+    far_all = list(range(4 * F, 4 * F + 4))
+    far = [[q for q in far_all if topo.same_plane(chip(q), chip(r))]]
+    far.append([q for q in far_all if q not in far[0]])
+    off = topo.engines(core, cores[mates[0]])
+    inner = [e for e in topo.engines(core, cores[partner]) if e not in off]
+    off_mask, in_mask, n_off, n_in = bits(off), bits(inner), len(off), len(inner)
+    half_a, half_b = bits(off[:n_off // 2]), bits(off[n_off // 2:])
+
+    rows = slice(64 * Q, 64 * Q + 64)
+    g.sync.dma_start(T.ct[0:64, :], T.tb[rows, 0:512]).then_inc(S.ct, 16)
+    g.sync.dma_start(T.ct[64:128, :], T.tb[rows, 512:1024]).then_inc(S.ct, 16)
+    for k in range(8):
+        g.sync.dma_start(T.xy[16 * k:16 * k + 16, 0:16], T.px[:, :]).then_inc(S.xy, 16)
+        g.scalar.dma_start(T.xy[16 * k:16 * k + 16, 16:32], T.py[:, :]).then_inc(S.xy, 16)
+    g.scalar.dma_start(T.st[0:64, :], T.tb[rows, :]).then_inc(S.st, 16)
+    g.scalar.dma_start(T.st[64:128, :], T.tb[rows, :]).then_inc(S.st, 16)
+    frows = slice(64 * F, 64 * F + 64)
+    g.sync.dma_start(T.sn0[0:64, :], T.w[rows, :]).then_inc(S.wn, 16)
+    g.sync.dma_start(T.sn1[64:128, :], T.w[rows, :]).then_inc(S.wn, 16)
+    g.sync.dma_start(T.sf0[0:64, :], T.w[frows, :]).then_inc(S.wf, 16)
+    g.sync.dma_start(T.sf1[64:128, :], T.w[frows, :]).then_inc(S.wf, 16)
+
+    lo = [0]
+
+    def send(transfers, n):
+        g.remote_dma_fused(transfers, local_sem=S.lo)
+        lo[0] += n
+
+    def xfer(dests, mask, sem, src, to):
+        return RemoteDMATransfer(dst_ids=[dst(q) for q in dests], dma_engine_mask=mask, remote_sem=sem,
+                                 srcs=[src], dsts=[to for q in dests], alu_op=0)
+
+    g.iota(T.pi[:, 0:1], [[0, 1]], 0, 1).then_inc(S["io_"], 1)
+
+    def send_far(e):
+        a = 256 * e + 128 * idx
+        send([xfer(far[e], off_mask, S["far%d" % e], T.cq[:, 0:128].bitcast(dt.uint8), T.farq[:, a:a + 128].bitcast(dt.uint8))], n_off)
+        send([xfer(far[e], off_mask, S["far%d" % e], T.cs[:, 0:128], T.fars[:, a:a + 128])], n_off)
+
+    g.wait_ge(S.tq, 1)
+    send_far(0)
+    g.wait_ge(S.on, 1)
+    to = T.arr[:, 8 * slot:8 * slot + 8]
+    send([xfer(mates, off_mask, S["a%d" % slot], T.offn[:, 0:8], to),
+          xfer([partner], in_mask, S["a%d" % slot], T.offn[:, 0:8], to)], n_off + n_in)
+    send_far(1)
+
+    def near_x(q, mask, plane):
+        s = q % 4
+        a, b = 128 * s, 128 * slot
+        if plane:
+            return xfer([q], mask, S["n%d" % slot], T.es[:, a:a + 128], T.nears[:, b:b + 128])
+        return xfer([q], mask, S["n%d" % slot], T.eq[:, a:a + 128].bitcast(dt.uint8), T.nearq[:, b:b + 128].bitcast(dt.uint8))
+
+    g.wait_ge(S["eq%d" % (partner % 4)], 1)
+    send([near_x(partner, in_mask, False)], n_in)
+    send([near_x(partner, in_mask, True)], n_in)
+    for q in mates:
+        g.wait_ge(S["eq%d" % (q % 4)], 1)
+    for plane in (False, True):
+        send([near_x(mates[0], half_a, plane), near_x(mates[1], half_b, plane)], n_off)
+    g.wait_ge(S.lo, lo[0])
+
+    def near_count(q):
+        return 2 * (n_in if q == partner else n_off // 2)
+
+    v = g.vector
+    vn = [0]
+
+    def V(i):
+        i.then_inc(S.v, 1)
+        vn[0] += 1
+
+    def vsync():
+        v.wait_ge(S.v, vn[0])
+
+    v.memset(T.zt[:, :], 0.0).then_inc(S.zt, 1)
+    v.wait_ge(S["io_"], 1)
+    V(v.tensor_scalar(T.gi[:, 0:1], T.pi[:, 0:1], 4, 3, shr, band))
+    vsync()
+    for k in range(4):
+        l = 4 * Q + k
+        for m, val in enumerate(((2 ** SH[l] - 1) / 2, 2.0 ** -SH[l], float(A[l]), float(B[l]))):
+            V(v.tensor_scalar(T.kt[:, 4 * k + m:4 * k + m + 1], T.gi[:, 0:1], float(k), val, AluOpType.is_equal, mult))
+    vsync()
+    V(v.tensor_tensor(T.ka[:, 0:8], T.kt[:, 0:8], T.kt[:, 8:16], add))
+    vsync()
+    V(v.tensor_tensor(T.kc[:, 0:4], T.ka[:, 0:4], T.ka[:, 4:8], add))
+    V(v.memset(T.sn0[64:128, 0:1024], 0.0))
+    v.wait_ge(S.ct, 32)
+    v.quantize_mx(T.cq[:, 0:128], T.cs[:, 0:128], T.ct[:, 0:512]).then_inc(S.tq, 1)
+    v.wait_ge(S.xy, 256)
+    vsync()
+    for h in range(2):
+        p = slice(64 * h, 64 * h + 64)
+        for m in range(2):
+            V(v.tensor_scalar(T.un[p, 8 * m:8 * m + 8], T.xy[p, 16 * m + 8 * h:16 * m + 8 * h + 8],
+                              T.kc[p, 0:1], T.kc[p, 1:2], sub, mult))
+    vsync()
+    for m in range(2):
+        V(v.tensor_scalar(T.mn[:, 8 * m:8 * m + 8], T.un[:, 8 * m:8 * m + 8], T.kc[:, 2 + m:3 + m], None, mult))
+    vsync()
+    V(v.tensor_tensor(T.an[:, 0:8], T.mn[:, 0:8], T.mn[:, 8:16], add))
+    vsync()
+    V(v.tensor_scalar(T.bn[:, 0:8], T.an[:, 0:8], 255, None, band))
+    vsync()
+    v.tensor_copy(T.offn[:, 0:8], T.bn[:, 0:8]).then_inc(S.on, 1)
+    V(v.memset(T.sn0[64:128, 1024:2048], 0.0))
+    V(v.memset(T.sn1[0:64, 0:2048], 0.0))
+    order = [q for e in range(2) for q in far[e]]
+    for k, l in enumerate(order):
+        V(v.tensor_scalar(T.uf[:, 32 * k:32 * k + 32], T.xy[:, 0:32], SH[l], None, shr))
+    vsync()
+    for k, l in enumerate(order):
+        V(v.tensor_scalar(T.mf[:, 16 * k:16 * k + 16], T.uf[:, 32 * k:32 * k + 16], float(A[l]), None, mult))
+        V(v.tensor_scalar(T.mf[:, 64 + 16 * k:80 + 16 * k], T.uf[:, 32 * k + 16:32 * k + 32], float(B[l]), None, mult))
+    vsync()
+    V(v.tensor_tensor(T.sf[:, 0:64], T.mf[:, 0:64], T.mf[:, 64:128], add))
+    vsync()
+    V(v.tensor_scalar(T.af[:, 0:64], T.sf[:, 0:64], 255, None, band))
+    V(v.tensor_scalar(T.hf[:, 0:64], T.sf[:, 0:64], 128, None, band))
+    vsync()
+    V(v.tensor_tensor(T.bf[:, 0:64], T.af[:, 0:64], T.hf[:, 0:64], add))
+    vsync()
+    for k in range(4):
+        for o in range(2):
+            a = 32 * k + 16 * o
+            V(v.tensor_scalar(T.offf[:, a:a + 16], T.bf[:, 16 * k:16 * k + 16], float(128 * (k % 2) + 512 * o), None, add))
+    v.wait_ge(S.wn, 32)
+    vsync()
+    v.quantize_mx(T.sn0q[:, 0:512], T.sn0s[:, 0:512], T.sn0[:, 0:2048]).then_inc(S.sn, 1)
+    v.quantize_mx(T.sn1q[:, 0:512], T.sn1s[:, 0:512], T.sn1[:, 0:2048]).then_inc(S.sn, 1)
+    v.wait_ge(S.wf, 32)
+    v.wait_ge(S.zf, 8)
+    v.quantize_mx(T.sf0q[:, 0:512], T.sf0s[:, 0:512], T.sf0[:, 0:2048]).then_inc(S.sf, 1)
+    v.quantize_mx(T.sf1q[:, 0:512], T.sf1s[:, 0:512], T.sf1[:, 0:2048]).then_inc(S.sf, 1)
+
+    near_order = [r, partner] + mates
+
+    def off_of(q):
+        return T.offn[:, 0:8] if q == r else T.arr[:, 8 * (q % 4):8 * (q % 4) + 8]
+
+    def wait_list(queue, q):
+        if q == r:
+            queue.wait_ge(S.on, 1)
+        else:
+            queue.wait_ge(S["a%d" % (q % 4)], n_in if q == partner else n_off)
+
+    v.wait_ge(S.sp, 4)
+    for q in near_order:
+        s = q % 4
+        wait_list(v, q)
+        for t in (2, 3):
+            v.tensor_copy(T["e%d" % s][:, t:512:4], T.wn[:, 256 * t:256 * t + 256].indirect(off_of(q))).then_inc(S["gv%d" % s], 1)
+        v.wait_ge(S["gv%d" % s], 2)
+        v.wait_ge(S["gs%d" % s], 2)
+        a = 128 * s
+        if q == r:
+            v.quantize_mx(T.nearq[:, a:a + 128], T.nears[:, a:a + 128], T["e%d" % s][:, 0:512]).then_inc(S["eq%d" % s], 1)
+        else:
+            v.quantize_mx(T.eq[:, a:a + 128], T.es[:, a:a + 128], T["e%d" % s][:, 0:512]).then_inc(S["eq%d" % s], 1)
+    for e in range(2):
+        pw = T["pw%d" % e]
+        for oo in range(2):
+            for b in range(4):
+                v.wait_ge(S["k%d%d%d" % (e, oo, b)], 1)
+            out = T.acc[:, 512 * oo:512 * oo + 512]
+            for i in range(2):
+                k = 2 * e + i
+                win = pw[:, 1024 * oo:1024 * oo + 1024].indirect(T.offf[:, 32 * k:32 * k + 32])
+                vsync()
+                if e == 0 and i == 0:
+                    V(v.tensor_copy(out, win))
+                else:
+                    V(v.tensor_tensor(out, win, out, add))
+    vsync()
+    for oo in range(2):
+        for b in range(4):
+            v.wait_ge(S["f%d%d" % (oo, b)], 1)
+            c = 512 * oo + 256 * (b // 2) + 128 * (b % 2)
+            bank = 512 * (4 + b if oo == 0 else b)
+            v.tensor_tensor(T.yo[:, c:c + 128], T.ps[:, bank:bank + 128], T.acc[:, c:c + 128], add).then_inc(S["y%d" % oo], 1)
+
+    sc = g.scalar
+    sc.wait_ge(S.zt, 1)
+    for k in range(4):
+        sc.activation(T.sf0[64:128, 512 * k:512 * k + 512], T.zt[64:128, :], copy).then_inc(S.zf, 1)
+    for k in range(4):
+        sc.activation(T.sf1[0:64, 512 * k:512 * k + 512], T.zt[0:64, :], copy).then_inc(S.zf, 1)
+    sc.wait_ge(S.st, 32)
+    for t in range(4):
+        sc.activation(T.wn[:, 256 * t:256 * t + 256], T.st[:, t:1024:4], copy).then_inc(S.sp, 1)
+    sc.wait_ge(S.sp, 4)
+    for q in near_order:
+        s = q % 4
+        wait_list(sc, q)
+        for t in (0, 1):
+            sc.activation(T["e%d" % s][:, t:512:4], T.wn[:, 256 * t:256 * t + 256].indirect(off_of(q)), copy).then_inc(S["gs%d" % s], 1)
+    for e in range(2):
+        for oo in range(2):
+            for b in range(4):
+                sc.wait_ge(S["p%d%d%d" % (e, oo, b)], 1)
+                a = 1024 * oo + 256 * b
+                sc.activation(T["pw%d" % e][:, a:a + 256], T.ps[:, 512 * b:512 * b + 256], copy).then_inc(S["k%d%d%d" % (e, oo, b)], 1)
+
+    te = g.tensor
+
+    def near(q, oo):
+        a = 128 * (q % 4)
+        for b in range(4):
+            o, h = 2 * oo + b // 2, b % 2
+            bank = 512 * (4 + b if oo == 0 else b)
+            w = slice(128 * o, 128 * o + 128)
+            i = te.matmul_mx(T.ps[:, bank:bank + 128], T["sn%dq" % h][:, w], T["sn%ds" % h][:, w],
+                             T.nearq[:, a:a + 128], T.nears[:, a:a + 128], q == near_order[0], q == near_order[-1])
+            if q == near_order[-1]:
+                i.then_inc(S["f%d%d" % (oo, b)], 1)
+
+    def far_products(e):
+        for oo in range(2):
+            for b in range(4):
+                o, h = 2 * oo + b // 2, b % 2
+                if (e, oo) != (0, 0):
+                    te.wait_ge(S["k%d%d%d" % ((e, 0, b) if oo else (e - 1, 1, b))], 1)
+                w = slice(128 * o, 128 * o + 128)
+                te.matmul_mx(T.ps[:, 512 * b:512 * b + 256], T["sf%dq" % h][:, w], T["sf%ds" % h][:, w],
+                             T.farq[:, 256 * e:256 * e + 256], T.fars[:, 256 * e:256 * e + 256], True, True).then_inc(S["p%d%d%d" % (e, oo, b)], 1)
+
+    te.wait_ge(S.sn, 2)
+    te.wait_ge(S["eq%d" % slot], 1)
+    near(r, 0)
+    te.wait_ge(S.sf, 2)
+    te.wait_ge(S.far0, 4 * n_off)
+    far_products(0)
+    te.wait_ge(S["n%d" % (partner % 4)], near_count(partner))
+    near(partner, 0)
+    te.wait_ge(S.far1, 4 * n_off)
+    far_products(1)
+    for q in mates:
+        te.wait_ge(S["n%d" % (q % 4)], near_count(q))
+        near(q, 0)
+    for b in range(4):
+        te.wait_ge(S["k11%d" % b], 1)
+    for q in near_order:
+        near(q, 1)
+
+    for oo in range(2):
+        g.sync.wait_ge(S["y%d" % oo], 4)
+        g.sync.dma_start(T.y[:, 512 * oo:512 * oo + 512], T.yo[:, 512 * oo:512 * oo + 512]).then_inc(S.yd, 16)
+    g.sync.wait_ge(S.yd, 32)

@@ -7,39 +7,32 @@ B = (1013, 1741, 587, 1459, 1907, 733, 1229, 1667)
 BF, F32, I32, U16, X4, U8 = "bfloat16", "float32", "int32", "uint16", "float8_e4m3fn_x4", "uint8"
 
 SCRATCH = {
-    "ct": ("sbuf", [128, 512], BF),
     "st": ("sbuf", [128, 1024], BF),
     "wn": ("sbuf", [128, 1024], BF),
     "zt": ("sbuf", [128, 512], BF),
-    "sn0": ("sbuf", [128, 2048], BF), "sn1": ("sbuf", [128, 2048], BF),
-    "sf0": ("sbuf", [128, 2048], BF), "sf1": ("sbuf", [128, 2048], BF),
-    "xy": ("sbuf", [128, 32], I32),
-    "pi": ("sbuf", [128, 1], I32), "gi": ("sbuf", [128, 1], I32),
-    "kt": ("sbuf", [128, 16], F32), "ka": ("sbuf", [128, 8], F32), "kc": ("sbuf", [128, 4], F32),
-    "un": ("sbuf", [128, 16], I32), "mn": ("sbuf", [128, 16], I32), "an": ("sbuf", [128, 8], I32),
-    "bn": ("sbuf", [128, 8], I32), "offn": ("sbuf", [128, 8], U16),
-    "uf": ("sbuf", [128, 128], I32), "mf": ("sbuf", [128, 128], I32), "sf": ("sbuf", [128, 64], I32),
-    "af": ("sbuf", [128, 64], I32), "hf": ("sbuf", [128, 64], I32), "bf": ("sbuf", [128, 64], I32),
-    "offf": ("sbuf", [128, 128], U16),
-    "arr": ("sbuf", [128, 32], U16),
-    "cq": ("sbuf", [128, 128], X4), "cs": ("sbuf", [128, 128], U8),
-    "eq": ("sbuf", [128, 512], X4), "es": ("sbuf", [128, 512], U8),
-    "farq": ("sbuf", [128, 512], X4), "fars": ("sbuf", [128, 512], U8),
-    "nearq": ("sbuf", [128, 512], X4), "nears": ("sbuf", [128, 512], U8),
-    "pw0": ("sbuf", [128, 2048], F32), "pw1": ("sbuf", [128, 2048], F32),
-    "acc": ("sbuf", [128, 1024], F32), "yo": ("sbuf", [128, 1024], F32),
+    "wx": ("sbuf", [128, 2048], BF),
+    "wy": ("sbuf", [128, 2048], BF),
+    "xy": ("sbuf", [128, 16], I32),
+    "pi": ("sbuf", [128, 8], I32), "b0": ("sbuf", [128, 8], I32), "b1": ("sbuf", [128, 1], I32),
+    "kt": ("sbuf", [128, 16], F32), "ke": ("sbuf", [128, 4], F32),
+    "ab": ("sbuf", [128, 32], I32), "un": ("sbuf", [128, 32], I32), "mn": ("sbuf", [128, 32], I32),
+    "an": ("sbuf", [128, 16], I32), "bn": ("sbuf", [128, 16], I32),
+    "off0": ("sbuf", [128, 8], U16), "off1": ("sbuf", [128, 8], U16),
+    "arr": ("sbuf", [128, 64], U16),
+    "e": ("sbuf", [128, 4096], BF),
+    "eq": ("sbuf", [128, 1024], X4), "es": ("sbuf", [128, 1024], U8),
+    "rq": ("sbuf", [128, 1024], X4), "rs": ("sbuf", [128, 1024], U8),
+    "yo": ("sbuf", [128, 1024], F32),
     "ps": ("psum", [128, 4096], F32),
 }
-for _n in ("sn0", "sn1", "sf0", "sf1"):
+for _n in ("s00", "s01", "s10", "s11"):
     SCRATCH[_n + "q"] = ("sbuf", [128, 512], X4)
     SCRATCH[_n + "s"] = ("sbuf", [128, 512], U8)
-for _s in range(4):
-    SCRATCH["e%d" % _s] = ("sbuf", [128, 512], BF)
 
-SEMAPHORES = ["v", "io_", "ct", "xy", "st", "wn", "wf", "zt", "zf", "tq", "on", "sp", "sn", "sf", "lo", "far0", "far1", "yd"]
-SEMAPHORES += ["%s%d" % (n, s) for n in ("a", "n", "gs", "gv", "eq") for s in range(4)]
-SEMAPHORES += ["%s%d%d%d" % (n, e, oo, b) for n in ("p", "k") for e in range(2) for oo in range(2) for b in range(4)]
-SEMAPHORES += ["f%d%d" % (oo, b) for oo in range(2) for b in range(4)] + ["y0", "y1"]
+SEMAPHORES = ["v", "io_", "xy", "st", "zt", "zs", "wx", "wy", "fx", "fy", "on0", "on1", "go", "sp", "lo", "yd"]
+SEMAPHORES += ["q00", "q01", "q10", "q11"]
+SEMAPHORES += ["%s%d" % (n, s) for n in ("a", "n", "gs", "gv", "eq", "f") for s in range(8)]
+SEMAPHORES += ["y%d" % o for o in range(4)]
 
 
 def rank_program(g, core, T, topo):
@@ -48,9 +41,9 @@ def rank_program(g, core, T, topo):
         return
     S = T.sem
     cores = list(T.cores)
-    Q, F, slot = r // 4, 1 - r // 4, r % 4
+    Q, F = r // 4, 1 - r // 4
     copy = ActivationFunctionType.Copy
-    add, sub, mult = AluOpType.add, AluOpType.subtract, AluOpType.mult
+    add, mult = AluOpType.add, AluOpType.mult
     shr, band = AluOpType.arith_shift_right, AluOpType.bitwise_and
 
     def chip(q):
@@ -67,27 +60,36 @@ def rank_program(g, core, T, topo):
     idx = same_chip.index(r)
     partner = [q for q in same_chip if q != r][0]
     mates = [q for q in range(4 * Q, 4 * Q + 4) if q not in same_chip]
+    mates = [mates[idx], mates[1 - idx]]
     far_all = list(range(4 * F, 4 * F + 4))
-    far = [[q for q in far_all if topo.same_plane(chip(q), chip(r))]]
-    far.append([q for q in far_all if q not in far[0]])
+    far1 = [q for q in far_all if topo.same_plane(chip(q), chip(r))]
+    far2 = [q for q in far_all if q not in far1]
     off = topo.engines(core, cores[mates[0]])
     inner = [e for e in topo.engines(core, cores[partner]) if e not in off]
     off_mask, in_mask, n_off, n_in = bits(off), bits(inner), len(off), len(inner)
     half_a, half_b = bits(off[:n_off // 2]), bits(off[n_off // 2:])
 
-    rows = slice(64 * Q, 64 * Q + 64)
-    g.sync.dma_start(T.ct[0:64, :], T.tb[rows, 0:512]).then_inc(S.ct, 16)
-    g.sync.dma_start(T.ct[64:128, :], T.tb[rows, 512:1024]).then_inc(S.ct, 16)
+    units = [([r], (3,)), ([partner], (3,)), (far2, (3,)), (far1, (3,)), ([mates[0]], (3,)), ([mates[1]], (2, 3))]
+
+    near_rows, far_rows = slice(64 * Q, 64 * Q + 64), slice(64 * F, 64 * F + 64)
     for k in range(8):
-        g.sync.dma_start(T.xy[16 * k:16 * k + 16, 0:16], T.px[:, :]).then_inc(S.xy, 16)
-        g.scalar.dma_start(T.xy[16 * k:16 * k + 16, 16:32], T.py[:, :]).then_inc(S.xy, 16)
-    g.scalar.dma_start(T.st[0:64, :], T.tb[rows, :]).then_inc(S.st, 16)
-    g.scalar.dma_start(T.st[64:128, :], T.tb[rows, :]).then_inc(S.st, 16)
-    frows = slice(64 * F, 64 * F + 64)
-    g.sync.dma_start(T.sn0[0:64, :], T.w[rows, :]).then_inc(S.wn, 16)
-    g.sync.dma_start(T.sn1[64:128, :], T.w[rows, :]).then_inc(S.wn, 16)
-    g.sync.dma_start(T.sf0[0:64, :], T.w[frows, :]).then_inc(S.wf, 16)
-    g.sync.dma_start(T.sf1[64:128, :], T.w[frows, :]).then_inc(S.wf, 16)
+        h = k // 4
+        g.sync.dma_start(T.xy[16 * k:16 * k + 16, 0:8], T.px[:, 8 * h:8 * h + 8]).then_inc(S.xy, 16)
+        g.scalar.dma_start(T.xy[16 * k:16 * k + 16, 8:16], T.py[:, 8 * h:8 * h + 8]).then_inc(S.xy, 16)
+    g.sync.dma_start(T.st[0:64, :], T.tb[near_rows, :]).then_inc(S.st, 16)
+    g.scalar.dma_start(T.st[64:128, :], T.tb[near_rows, :]).then_inc(S.st, 16)
+    g.sync.dma_start(T.wx[0:64, :], T.w[near_rows, :]).then_inc(S.wx, 16)
+    g.sync.wait_ge(S.zt, 1)
+    for k in (1, 2, 3):
+        g.sync.dma_start(T.wx[64:128, 512 * k:512 * k + 512], T.zt[64:128, :]).then_inc(S.wx, 16)
+    g.sync.wait_ge(S.go, 1)
+    g.sync.dma_start(T.wy[64:128, :], T.w[near_rows, :]).then_inc(S.wy, 16)
+    for k in (2, 3):
+        g.sync.dma_start(T.wy[0:64, 512 * k:512 * k + 512], T.zt[0:64, :]).then_inc(S.wy, 16)
+    g.sync.wait_ge(S["q%d0" % Q], 1)
+    g.sync.dma_start(T.wx[0:64, :], T.w[far_rows, :]).then_inc(S.fx, 16)
+    g.sync.wait_ge(S["q%d1" % Q], 1)
+    g.sync.dma_start(T.wy[64:128, :], T.w[far_rows, :]).then_inc(S.fy, 16)
 
     lo = [0]
 
@@ -99,39 +101,35 @@ def rank_program(g, core, T, topo):
         return RemoteDMATransfer(dst_ids=[dst(q) for q in dests], dma_engine_mask=mask, remote_sem=sem,
                                  srcs=[src], dsts=[to for q in dests], alu_op=0)
 
-    g.iota(T.pi[:, 0:1], [[0, 1]], 0, 1).then_inc(S["io_"], 1)
+    g.iota(T.pi[:, 0:8], [[0, 8]], 0, 1).then_inc(S["io_"], 1)
+    slot = T.arr[:, 8 * r:8 * r + 8]
+    own = T["off%d" % Q]
+    g.wait_ge(S["on%d" % F], 1)
+    send([xfer(far2 + far1, off_mask, S["a%d" % r], T["off%d" % F][:, 0:8], slot)], n_off)
+    g.wait_ge(S["on%d" % Q], 1)
+    send([xfer(mates, off_mask, S["a%d" % r], own[:, 0:8], slot),
+          xfer([partner], in_mask, S["a%d" % r], own[:, 0:8], slot)], n_off + n_in)
+    g.sem_inc(S.go)
 
-    def send_far(e):
-        a = 256 * e + 128 * idx
-        send([xfer(far[e], off_mask, S["far%d" % e], T.cq[:, 0:128].bitcast(dt.uint8), T.farq[:, a:a + 128].bitcast(dt.uint8))], n_off)
-        send([xfer(far[e], off_mask, S["far%d" % e], T.cs[:, 0:128], T.fars[:, a:a + 128])], n_off)
-
-    g.wait_ge(S.tq, 1)
-    send_far(0)
-    g.wait_ge(S.on, 1)
-    to = T.arr[:, 8 * slot:8 * slot + 8]
-    send([xfer(mates, off_mask, S["a%d" % slot], T.offn[:, 0:8], to),
-          xfer([partner], in_mask, S["a%d" % slot], T.offn[:, 0:8], to)], n_off + n_in)
-    send_far(1)
-
-    def near_x(q, mask, plane):
-        s = q % 4
-        a, b = 128 * s, 128 * slot
+    def codes(q, mask, plane):
+        a, b = 128 * q, 128 * r
         if plane:
-            return xfer([q], mask, S["n%d" % slot], T.es[:, a:a + 128], T.nears[:, b:b + 128])
-        return xfer([q], mask, S["n%d" % slot], T.eq[:, a:a + 128].bitcast(dt.uint8), T.nearq[:, b:b + 128].bitcast(dt.uint8))
+            return xfer([q], mask, S["n%d" % r], T.es[:, a:a + 128], T.rs[:, b:b + 128])
+        return xfer([q], mask, S["n%d" % r], T.eq[:, a:a + 128].bitcast(dt.uint8), T.rq[:, b:b + 128].bitcast(dt.uint8))
 
-    g.wait_ge(S["eq%d" % (partner % 4)], 1)
-    send([near_x(partner, in_mask, False)], n_in)
-    send([near_x(partner, in_mask, True)], n_in)
-    for q in mates:
-        g.wait_ge(S["eq%d" % (q % 4)], 1)
-    for plane in (False, True):
-        send([near_x(mates[0], half_a, plane), near_x(mates[1], half_b, plane)], n_off)
+    for qs, _ in units[1:]:
+        g.wait_ge(S["eq%d" % qs[0]], 1)
+        for plane in (False, True):
+            if len(qs) == 2:
+                send([codes(qs[0], half_a, plane), codes(qs[1], half_b, plane)], n_off)
+            elif qs[0] == partner:
+                send([codes(partner, in_mask, plane)], n_in)
+            else:
+                send([codes(qs[0], off_mask, plane)], n_off)
     g.wait_ge(S.lo, lo[0])
 
-    def near_count(q):
-        return 2 * (n_in if q == partner else n_off // 2)
+    def arrivals(q):
+        return 2 * (n_in if q == partner else n_off if q in mates else n_off // 2)
 
     v = g.vector
     vn = [0]
@@ -145,175 +143,136 @@ def rank_program(g, core, T, topo):
 
     v.memset(T.zt[:, :], 0.0).then_inc(S.zt, 1)
     v.wait_ge(S["io_"], 1)
-    V(v.tensor_scalar(T.gi[:, 0:1], T.pi[:, 0:1], 4, 3, shr, band))
+    V(v.tensor_scalar(T.b1[:, 0:1], T.pi[:, 0:1], 5, 1, shr, band))
+    V(v.tensor_scalar(T.b0[:, 0:8], T.pi[:, 0:8], 4, 1, shr, band))
     vsync()
-    for k in range(4):
-        l = 4 * Q + k
-        for m, val in enumerate(((2 ** SH[l] - 1) / 2, 2.0 ** -SH[l], float(A[l]), float(B[l]))):
-            V(v.tensor_scalar(T.kt[:, 4 * k + m:4 * k + m + 1], T.gi[:, 0:1], float(k), val, AluOpType.is_equal, mult))
+    c = 2.0 ** -SH[0]
+    V(v.tensor_scalar(T.kt[:, 0:1], T.b1[:, 0:1], 3 * c, c, mult, add))
+    tabs = [(m, s, (A, B)[m][4 * s:4 * s + 4]) for m in range(2) for s in range(2)]
+    for i, (m, s, z) in enumerate(tabs):
+        V(v.tensor_scalar(T.kt[:, 2 * i + 2:2 * i + 3], T.b1[:, 0:1], float(z[3] - z[2] - z[1] + z[0]), float(z[1] - z[0]), mult, add))
+        V(v.tensor_scalar(T.kt[:, 2 * i + 3:2 * i + 4], T.b1[:, 0:1], float(z[2] - z[0]), float(z[0]), mult, add))
     vsync()
-    V(v.tensor_tensor(T.ka[:, 0:8], T.kt[:, 0:8], T.kt[:, 8:16], add))
+    V(v.tensor_scalar(T.ke[:, 0:1], T.b0[:, 0:1], T.kt[:, 0:1], T.kt[:, 0:1], mult, add))
+    for i, (m, s, z) in enumerate(tabs):
+        V(v.tensor_scalar(T.ab[:, 16 * m + s:16 * m + 16:2], T.b0[:, 0:8], T.kt[:, 2 * i + 2:2 * i + 3], T.kt[:, 2 * i + 3:2 * i + 4], mult, add))
     vsync()
-    V(v.tensor_tensor(T.kc[:, 0:4], T.ka[:, 0:4], T.ka[:, 4:8], add))
-    V(v.memset(T.sn0[64:128, 0:1024], 0.0))
-    v.wait_ge(S.ct, 32)
-    v.quantize_mx(T.cq[:, 0:128], T.cs[:, 0:128], T.ct[:, 0:512]).then_inc(S.tq, 1)
+    V(v.tensor_scalar(T.ke[:, 1:2], T.ke[:, 0:1], 0.5, -0.5, mult, add))
+    V(v.tensor_scalar(T.ke[:, 2:3], T.ke[:, 0:1], 16.0, None, mult))
+    V(v.tensor_scalar(T.ke[:, 3:4], T.ke[:, 0:1], 8.0, -0.5, mult, add))
     v.wait_ge(S.xy, 256)
     vsync()
-    for h in range(2):
-        p = slice(64 * h, 64 * h + 64)
-        for m in range(2):
-            V(v.tensor_scalar(T.un[p, 8 * m:8 * m + 8], T.xy[p, 16 * m + 8 * h:16 * m + 8 * h + 8],
-                              T.kc[p, 0:1], T.kc[p, 1:2], sub, mult))
+    for s in range(2):
+        V(v.tensor_scalar(T.un[:, s:32:2], T.xy[:, 0:16], T.ke[:, 2 * s:2 * s + 1], T.ke[:, 2 * s + 1:2 * s + 2], mult, add))
     vsync()
-    for m in range(2):
-        V(v.tensor_scalar(T.mn[:, 8 * m:8 * m + 8], T.un[:, 8 * m:8 * m + 8], T.kc[:, 2 + m:3 + m], None, mult))
+    V(v.tensor_tensor(T.mn[:, 0:32], T.un[:, 0:32], T.ab[:, 0:32], mult))
     vsync()
-    V(v.tensor_tensor(T.an[:, 0:8], T.mn[:, 0:8], T.mn[:, 8:16], add))
+    V(v.tensor_tensor(T.an[:, 0:16], T.mn[:, 0:16], T.mn[:, 16:32], add))
     vsync()
-    V(v.tensor_scalar(T.bn[:, 0:8], T.an[:, 0:8], 255, None, band))
+    V(v.tensor_scalar(T.bn[:, 0:16], T.an[:, 0:16], 255, None, band))
     vsync()
-    v.tensor_copy(T.offn[:, 0:8], T.bn[:, 0:8]).then_inc(S.on, 1)
-    V(v.memset(T.sn0[64:128, 1024:2048], 0.0))
-    V(v.memset(T.sn1[0:64, 0:2048], 0.0))
-    order = [q for e in range(2) for q in far[e]]
-    for k, l in enumerate(order):
-        V(v.tensor_scalar(T.uf[:, 32 * k:32 * k + 32], T.xy[:, 0:32], SH[l], None, shr))
-    vsync()
-    for k, l in enumerate(order):
-        V(v.tensor_scalar(T.mf[:, 16 * k:16 * k + 16], T.uf[:, 32 * k:32 * k + 16], float(A[l]), None, mult))
-        V(v.tensor_scalar(T.mf[:, 64 + 16 * k:80 + 16 * k], T.uf[:, 32 * k + 16:32 * k + 32], float(B[l]), None, mult))
-    vsync()
-    V(v.tensor_tensor(T.sf[:, 0:64], T.mf[:, 0:64], T.mf[:, 64:128], add))
-    vsync()
-    V(v.tensor_scalar(T.af[:, 0:64], T.sf[:, 0:64], 255, None, band))
-    V(v.tensor_scalar(T.hf[:, 0:64], T.sf[:, 0:64], 128, None, band))
-    vsync()
-    V(v.tensor_tensor(T.bf[:, 0:64], T.af[:, 0:64], T.hf[:, 0:64], add))
-    vsync()
-    for k in range(4):
-        for o in range(2):
-            a = 32 * k + 16 * o
-            V(v.tensor_scalar(T.offf[:, a:a + 16], T.bf[:, 16 * k:16 * k + 16], float(128 * (k % 2) + 512 * o), None, add))
-    v.wait_ge(S.wn, 32)
-    vsync()
-    v.quantize_mx(T.sn0q[:, 0:512], T.sn0s[:, 0:512], T.sn0[:, 0:2048]).then_inc(S.sn, 1)
-    v.quantize_mx(T.sn1q[:, 0:512], T.sn1s[:, 0:512], T.sn1[:, 0:2048]).then_inc(S.sn, 1)
-    v.wait_ge(S.wf, 32)
-    v.wait_ge(S.zf, 8)
-    v.quantize_mx(T.sf0q[:, 0:512], T.sf0s[:, 0:512], T.sf0[:, 0:2048]).then_inc(S.sf, 1)
-    v.quantize_mx(T.sf1q[:, 0:512], T.sf1s[:, 0:512], T.sf1[:, 0:2048]).then_inc(S.sf, 1)
+    for s in (F, Q):
+        v.tensor_copy(T["off%d" % s][:, 0:8], T.bn[:, s:16:2]).then_inc(S["on%d" % s], 1)
 
-    near_order = [r, partner] + mates
+    def stat(s, h, sem, n):
+        v.wait_ge(S[sem], n)
+        src = T.wx if h == 0 else T.wy
+        v.quantize_mx(T["s%d%dq" % (s, h)][:, 0:512], T["s%d%ds" % (s, h)][:, 0:512], src[:, 0:2048]).then_inc(S["q%d%d" % (s, h)], 1)
 
-    def off_of(q):
-        return T.offn[:, 0:8] if q == r else T.arr[:, 8 * (q % 4):8 * (q % 4) + 8]
+    def wait_lists(queue, qs):
+        for q in qs:
+            if q == r:
+                queue.wait_ge(S["on%d" % Q], 1)
+            else:
+                queue.wait_ge(S["a%d" % q], n_in if q == partner else n_off)
 
-    def wait_list(queue, q):
-        if q == r:
-            queue.wait_ge(S.on, 1)
-        else:
-            queue.wait_ge(S["a%d" % (q % 4)], n_in if q == partner else n_off)
+    def gather(call, qs, t, sem, *more):
+        q0, n = min(qs), len(qs)
+        lists = own[:, 0:8] if qs[0] == r else T.arr[:, 8 * q0:8 * (q0 + n)]
+        call(T.e[:, 512 * q0 + t:512 * (q0 + n):4], T.wn[:, 256 * t:256 * t + 256].indirect(lists), *more).then_inc(S["%s%d" % (sem, q0)], 1)
 
+    def vgather(u):
+        qs, ts = units[u]
+        wait_lists(v, qs)
+        for t in ts:
+            gather(v.tensor_copy, qs, t, "gv")
+
+    def pack(u):
+        qs, ts = units[u]
+        q0, n = min(qs), len(qs)
+        v.wait_ge(S["gv%d" % q0], len(ts))
+        v.wait_ge(S["gs%d" % q0], 4 - len(ts))
+        a, b = 128 * q0, 128 * (q0 + n)
+        cq, cs = (T.rq, T.rs) if q0 == r else (T.eq, T.es)
+        v.quantize_mx(cq[:, a:b], cs[:, a:b], T.e[:, 4 * a:4 * b]).then_inc(S["eq%d" % q0], 1)
+
+    v.wait_ge(S.zs, 1)
+    stat(Q, 0, "wx", 64)
+    V(v.memset(T.wy[0:64, 0:1024], 0.0))
     v.wait_ge(S.sp, 4)
-    for q in near_order:
-        s = q % 4
-        wait_list(v, q)
-        for t in (2, 3):
-            v.tensor_copy(T["e%d" % s][:, t:512:4], T.wn[:, 256 * t:256 * t + 256].indirect(off_of(q))).then_inc(S["gv%d" % s], 1)
-        v.wait_ge(S["gv%d" % s], 2)
-        v.wait_ge(S["gs%d" % s], 2)
-        a = 128 * s
-        if q == r:
-            v.quantize_mx(T.nearq[:, a:a + 128], T.nears[:, a:a + 128], T["e%d" % s][:, 0:512]).then_inc(S["eq%d" % s], 1)
-        else:
-            v.quantize_mx(T.eq[:, a:a + 128], T.es[:, a:a + 128], T["e%d" % s][:, 0:512]).then_inc(S["eq%d" % s], 1)
-    for e in range(2):
-        pw = T["pw%d" % e]
-        for oo in range(2):
-            for b in range(4):
-                v.wait_ge(S["k%d%d%d" % (e, oo, b)], 1)
-            out = T.acc[:, 512 * oo:512 * oo + 512]
-            for i in range(2):
-                k = 2 * e + i
-                win = pw[:, 1024 * oo:1024 * oo + 1024].indirect(T.offf[:, 32 * k:32 * k + 32])
-                vsync()
-                if e == 0 and i == 0:
-                    V(v.tensor_copy(out, win))
-                else:
-                    V(v.tensor_tensor(out, win, out, add))
+    vgather(0)
+    vgather(1)
+    pack(0)
     vsync()
-    for oo in range(2):
-        for b in range(4):
-            v.wait_ge(S["f%d%d" % (oo, b)], 1)
-            c = 512 * oo + 256 * (b // 2) + 128 * (b % 2)
-            bank = 512 * (4 + b if oo == 0 else b)
-            v.tensor_tensor(T.yo[:, c:c + 128], T.ps[:, bank:bank + 128], T.acc[:, c:c + 128], add).then_inc(S["y%d" % oo], 1)
+    stat(Q, 1, "wy", 48)
+    pack(1)
+    vgather(2)
+    stat(F, 0, "fx", 16)
+    pack(2)
+    vgather(3)
+    stat(F, 1, "fy", 16)
+    pack(3)
+    vgather(4)
+    pack(4)
+    vgather(5)
+    pack(5)
+
+    def finish(call, o, h, *more):
+        i = 2 * o + h
+        call(T.yo[:, 128 * i:128 * i + 128], T.ps[:, 512 * i:512 * i + 128], *more).then_inc(S["y%d" % o], 1)
+
+    for o in range(4):
+        v.wait_ge(S["f%d" % (2 * o + 1)], 1)
+        finish(v.tensor_copy, o, 1)
 
     sc = g.scalar
     sc.wait_ge(S.zt, 1)
-    for k in range(4):
-        sc.activation(T.sf0[64:128, 512 * k:512 * k + 512], T.zt[64:128, :], copy).then_inc(S.zf, 1)
-    for k in range(4):
-        sc.activation(T.sf1[0:64, 512 * k:512 * k + 512], T.zt[0:64, :], copy).then_inc(S.zf, 1)
+    sc.activation(T.wx[64:128, 0:512], T.zt[64:128, :], copy).then_inc(S.zs, 1)
     sc.wait_ge(S.st, 32)
     for t in range(4):
         sc.activation(T.wn[:, 256 * t:256 * t + 256], T.st[:, t:1024:4], copy).then_inc(S.sp, 1)
     sc.wait_ge(S.sp, 4)
-    for q in near_order:
-        s = q % 4
-        wait_list(sc, q)
-        for t in (0, 1):
-            sc.activation(T["e%d" % s][:, t:512:4], T.wn[:, 256 * t:256 * t + 256].indirect(off_of(q)), copy).then_inc(S["gs%d" % s], 1)
-    for e in range(2):
-        for oo in range(2):
-            for b in range(4):
-                sc.wait_ge(S["p%d%d%d" % (e, oo, b)], 1)
-                a = 1024 * oo + 256 * b
-                sc.activation(T["pw%d" % e][:, a:a + 256], T.ps[:, 512 * b:512 * b + 256], copy).then_inc(S["k%d%d%d" % (e, oo, b)], 1)
+    for qs, ts in units:
+        wait_lists(sc, qs)
+        for t in range(4):
+            if t not in ts:
+                gather(sc.activation, qs, t, "gs", copy)
+    for o in range(4):
+        sc.wait_ge(S["f%d" % (2 * o)], 1)
+        finish(sc.activation, o, 0, copy)
 
     te = g.tensor
-
-    def near(q, oo):
-        a = 128 * (q % 4)
-        for b in range(4):
-            o, h = 2 * oo + b // 2, b % 2
-            bank = 512 * (4 + b if oo == 0 else b)
+    order = [q for qs, _ in units for q in qs]
+    for q in order:
+        s = q // 4
+        if q == order[0]:
+            te.wait_ge(S["eq%d" % r], 1)
+            te.wait_ge(S["q%d0" % Q], 1)
+            te.wait_ge(S["q%d1" % Q], 1)
+        else:
+            if q == far2[0]:
+                te.wait_ge(S["q%d0" % F], 1)
+                te.wait_ge(S["q%d1" % F], 1)
+            te.wait_ge(S["n%d" % q], arrivals(q))
+        for i in range(8):
+            o, h = i // 2, i % 2
             w = slice(128 * o, 128 * o + 128)
-            i = te.matmul_mx(T.ps[:, bank:bank + 128], T["sn%dq" % h][:, w], T["sn%ds" % h][:, w],
-                             T.nearq[:, a:a + 128], T.nears[:, a:a + 128], q == near_order[0], q == near_order[-1])
-            if q == near_order[-1]:
-                i.then_inc(S["f%d%d" % (oo, b)], 1)
+            c = te.matmul_mx(T.ps[:, 512 * i:512 * i + 128], T["s%d%dq" % (s, h)][:, w], T["s%d%ds" % (s, h)][:, w],
+                             T.rq[:, 128 * q:128 * q + 128], T.rs[:, 128 * q:128 * q + 128], q == order[0], q == order[-1])
+            if q == order[-1]:
+                c.then_inc(S["f%d" % i], 1)
 
-    def far_products(e):
-        for oo in range(2):
-            for b in range(4):
-                o, h = 2 * oo + b // 2, b % 2
-                if (e, oo) != (0, 0):
-                    te.wait_ge(S["k%d%d%d" % ((e, 0, b) if oo else (e - 1, 1, b))], 1)
-                w = slice(128 * o, 128 * o + 128)
-                te.matmul_mx(T.ps[:, 512 * b:512 * b + 256], T["sf%dq" % h][:, w], T["sf%ds" % h][:, w],
-                             T.farq[:, 256 * e:256 * e + 256], T.fars[:, 256 * e:256 * e + 256], True, True).then_inc(S["p%d%d%d" % (e, oo, b)], 1)
-
-    te.wait_ge(S.sn, 2)
-    te.wait_ge(S["eq%d" % slot], 1)
-    near(r, 0)
-    te.wait_ge(S.sf, 2)
-    te.wait_ge(S.far0, 4 * n_off)
-    far_products(0)
-    te.wait_ge(S["n%d" % (partner % 4)], near_count(partner))
-    near(partner, 0)
-    te.wait_ge(S.far1, 4 * n_off)
-    far_products(1)
-    for q in mates:
-        te.wait_ge(S["n%d" % (q % 4)], near_count(q))
-        near(q, 0)
-    for b in range(4):
-        te.wait_ge(S["k11%d" % b], 1)
-    for q in near_order:
-        near(q, 1)
-
-    for oo in range(2):
-        g.sync.wait_ge(S["y%d" % oo], 4)
-        g.sync.dma_start(T.y[:, 512 * oo:512 * oo + 512], T.yo[:, 512 * oo:512 * oo + 512]).then_inc(S.yd, 16)
-    g.sync.wait_ge(S.yd, 32)
+    for o in range(4):
+        g.sync.wait_ge(S["y%d" % o], 2)
+        g.sync.dma_start(T.y[:, 256 * o:256 * o + 256], T.yo[:, 256 * o:256 * o + 256]).then_inc(S.yd, 16)
+    g.sync.wait_ge(S.yd, 64)

from concourse.bass import DstId, RemoteDMATransfer
from concourse.mybir import dt, AluOpType, ActivationFunctionType

SH = (7, 6, 5, 4, 3, 2, 1, 0)
A = (1531, 797, 1877, 1129, 619, 1993, 1367, 911)
B = (1013, 1741, 587, 1459, 1907, 733, 1229, 1667)
BF, F32, I32, U16, X4, U8 = "bfloat16", "float32", "int32", "uint16", "float8_e4m3fn_x4", "uint8"

SCRATCH = {
    "st": ("sbuf", [128, 1024], BF),
    "wn": ("sbuf", [128, 1024], BF),
    "zt": ("sbuf", [128, 512], BF),
    "wx": ("sbuf", [128, 2048], BF),
    "wy": ("sbuf", [128, 2048], BF),
    "xy": ("sbuf", [128, 16], I32),
    "pi": ("sbuf", [128, 8], I32), "b0": ("sbuf", [128, 8], I32), "b1": ("sbuf", [128, 1], I32),
    "kt": ("sbuf", [128, 16], F32), "ke": ("sbuf", [128, 4], F32),
    "ab": ("sbuf", [128, 32], I32), "un": ("sbuf", [128, 32], I32), "mn": ("sbuf", [128, 32], I32),
    "an": ("sbuf", [128, 16], I32), "bn": ("sbuf", [128, 16], I32),
    "off0": ("sbuf", [128, 8], U16), "off1": ("sbuf", [128, 8], U16),
    "arr": ("sbuf", [128, 64], U16),
    "e": ("sbuf", [128, 4096], BF),
    "eq": ("sbuf", [128, 1024], X4), "es": ("sbuf", [128, 1024], U8),
    "rq": ("sbuf", [128, 1024], X4), "rs": ("sbuf", [128, 1024], U8),
    "yo": ("sbuf", [128, 1024], F32),
    "ps": ("psum", [128, 4096], F32),
}
for _n in ("s00", "s01", "s10", "s11"):
    SCRATCH[_n + "q"] = ("sbuf", [128, 512], X4)
    SCRATCH[_n + "s"] = ("sbuf", [128, 512], U8)

SEMAPHORES = ["v", "io_", "xy", "st", "zt", "zs", "wx", "wy", "fx", "fy", "on0", "on1", "go", "sp", "lo", "yd"]
SEMAPHORES += ["q00", "q01", "q10", "q11"]
SEMAPHORES += ["%s%d" % (n, s) for n in ("a", "n", "gs", "gv", "eq", "f") for s in range(8)]
SEMAPHORES += ["y%d" % o for o in range(4)]


def rank_program(g, core, T, topo):
    r = T.rank_of(core)
    if r is None:
        return
    S = T.sem
    cores = list(T.cores)
    Q, F = r // 4, 1 - r // 4
    copy = ActivationFunctionType.Copy
    add, mult = AluOpType.add, AluOpType.mult
    shr, band = AluOpType.arith_shift_right, AluOpType.bitwise_and

    def chip(q):
        return topo.chip(cores[q])

    def dst(q):
        rid, pid, _ = topo.addr(cores[q])
        return DstId(rid=rid, pnc=pid)

    def bits(es):
        return sum(1 << e for e in es)

    same_chip = [q for q in range(8) if chip(q) == chip(r)]
    idx = same_chip.index(r)
    partner = [q for q in same_chip if q != r][0]
    mates = [q for q in range(4 * Q, 4 * Q + 4) if q not in same_chip]
    mates = [mates[idx], mates[1 - idx]]
    far_all = list(range(4 * F, 4 * F + 4))
    far1 = [q for q in far_all if topo.same_plane(chip(q), chip(r))]
    far2 = [q for q in far_all if q not in far1]
    off = topo.engines(core, cores[mates[0]])
    inner = [e for e in topo.engines(core, cores[partner]) if e not in off]
    off_mask, in_mask, n_off, n_in = bits(off), bits(inner), len(off), len(inner)
    half_a, half_b = bits(off[:n_off // 2]), bits(off[n_off // 2:])

    units = [([r], (3,)), ([partner], (3,)), (far2, (3,)), (far1, (3,)), ([mates[0]], (3,)), ([mates[1]], (2, 3))]

    near_rows, far_rows = slice(64 * Q, 64 * Q + 64), slice(64 * F, 64 * F + 64)
    for k in range(8):
        h = k // 4
        g.sync.dma_start(T.xy[16 * k:16 * k + 16, 0:8], T.px[:, 8 * h:8 * h + 8]).then_inc(S.xy, 16)
        g.scalar.dma_start(T.xy[16 * k:16 * k + 16, 8:16], T.py[:, 8 * h:8 * h + 8]).then_inc(S.xy, 16)
    g.sync.dma_start(T.st[0:64, :], T.tb[near_rows, :]).then_inc(S.st, 16)
    g.scalar.dma_start(T.st[64:128, :], T.tb[near_rows, :]).then_inc(S.st, 16)
    g.sync.dma_start(T.wx[0:64, :], T.w[near_rows, :]).then_inc(S.wx, 16)
    g.sync.wait_ge(S.zt, 1)
    for k in (1, 2, 3):
        g.sync.dma_start(T.wx[64:128, 512 * k:512 * k + 512], T.zt[64:128, :]).then_inc(S.wx, 16)
    g.sync.wait_ge(S.go, 1)
    g.sync.dma_start(T.wy[64:128, :], T.w[near_rows, :]).then_inc(S.wy, 16)
    for k in (2, 3):
        g.sync.dma_start(T.wy[0:64, 512 * k:512 * k + 512], T.zt[0:64, :]).then_inc(S.wy, 16)
    g.sync.wait_ge(S["q%d0" % Q], 1)
    g.sync.dma_start(T.wx[0:64, :], T.w[far_rows, :]).then_inc(S.fx, 16)
    g.sync.wait_ge(S["q%d1" % Q], 1)
    g.sync.dma_start(T.wy[64:128, :], T.w[far_rows, :]).then_inc(S.fy, 16)

    lo = [0]

    def send(transfers, n):
        g.remote_dma_fused(transfers, local_sem=S.lo)
        lo[0] += n

    def xfer(dests, mask, sem, src, to):
        return RemoteDMATransfer(dst_ids=[dst(q) for q in dests], dma_engine_mask=mask, remote_sem=sem,
                                 srcs=[src], dsts=[to for q in dests], alu_op=0)

    g.iota(T.pi[:, 0:8], [[0, 8]], 0, 1).then_inc(S["io_"], 1)
    slot = T.arr[:, 8 * r:8 * r + 8]
    own = T["off%d" % Q]
    g.wait_ge(S["on%d" % F], 1)
    send([xfer(far2 + far1, off_mask, S["a%d" % r], T["off%d" % F][:, 0:8], slot)], n_off)
    g.wait_ge(S["on%d" % Q], 1)
    send([xfer(mates, off_mask, S["a%d" % r], own[:, 0:8], slot),
          xfer([partner], in_mask, S["a%d" % r], own[:, 0:8], slot)], n_off + n_in)
    g.sem_inc(S.go)

    def codes(q, mask, plane):
        a, b = 128 * q, 128 * r
        if plane:
            return xfer([q], mask, S["n%d" % r], T.es[:, a:a + 128], T.rs[:, b:b + 128])
        return xfer([q], mask, S["n%d" % r], T.eq[:, a:a + 128].bitcast(dt.uint8), T.rq[:, b:b + 128].bitcast(dt.uint8))

    for qs, _ in units[1:]:
        g.wait_ge(S["eq%d" % qs[0]], 1)
        for plane in (False, True):
            if len(qs) == 2:
                send([codes(qs[0], half_a, plane), codes(qs[1], half_b, plane)], n_off)
            elif qs[0] == partner:
                send([codes(partner, in_mask, plane)], n_in)
            else:
                send([codes(qs[0], off_mask, plane)], n_off)
    g.wait_ge(S.lo, lo[0])

    def arrivals(q):
        return 2 * (n_in if q == partner else n_off if q in mates else n_off // 2)

    v = g.vector
    vn = [0]

    def V(i):
        i.then_inc(S.v, 1)
        vn[0] += 1

    def vsync():
        v.wait_ge(S.v, vn[0])

    v.memset(T.zt[:, :], 0.0).then_inc(S.zt, 1)
    v.wait_ge(S["io_"], 1)
    V(v.tensor_scalar(T.b1[:, 0:1], T.pi[:, 0:1], 5, 1, shr, band))
    V(v.tensor_scalar(T.b0[:, 0:8], T.pi[:, 0:8], 4, 1, shr, band))
    vsync()
    c = 2.0 ** -SH[0]
    V(v.tensor_scalar(T.kt[:, 0:1], T.b1[:, 0:1], 3 * c, c, mult, add))
    tabs = [(m, s, (A, B)[m][4 * s:4 * s + 4]) for m in range(2) for s in range(2)]
    for i, (m, s, z) in enumerate(tabs):
        V(v.tensor_scalar(T.kt[:, 2 * i + 2:2 * i + 3], T.b1[:, 0:1], float(z[3] - z[2] - z[1] + z[0]), float(z[1] - z[0]), mult, add))
        V(v.tensor_scalar(T.kt[:, 2 * i + 3:2 * i + 4], T.b1[:, 0:1], float(z[2] - z[0]), float(z[0]), mult, add))
    vsync()
    V(v.tensor_scalar(T.ke[:, 0:1], T.b0[:, 0:1], T.kt[:, 0:1], T.kt[:, 0:1], mult, add))
    for i, (m, s, z) in enumerate(tabs):
        V(v.tensor_scalar(T.ab[:, 16 * m + s:16 * m + 16:2], T.b0[:, 0:8], T.kt[:, 2 * i + 2:2 * i + 3], T.kt[:, 2 * i + 3:2 * i + 4], mult, add))
    vsync()
    V(v.tensor_scalar(T.ke[:, 1:2], T.ke[:, 0:1], 0.5, -0.5, mult, add))
    V(v.tensor_scalar(T.ke[:, 2:3], T.ke[:, 0:1], 16.0, None, mult))
    V(v.tensor_scalar(T.ke[:, 3:4], T.ke[:, 0:1], 8.0, -0.5, mult, add))
    v.wait_ge(S.xy, 256)
    vsync()
    for s in range(2):
        V(v.tensor_scalar(T.un[:, s:32:2], T.xy[:, 0:16], T.ke[:, 2 * s:2 * s + 1], T.ke[:, 2 * s + 1:2 * s + 2], mult, add))
    vsync()
    V(v.tensor_tensor(T.mn[:, 0:32], T.un[:, 0:32], T.ab[:, 0:32], mult))
    vsync()
    V(v.tensor_tensor(T.an[:, 0:16], T.mn[:, 0:16], T.mn[:, 16:32], add))
    vsync()
    V(v.tensor_scalar(T.bn[:, 0:16], T.an[:, 0:16], 255, None, band))
    vsync()
    for s in (F, Q):
        v.tensor_copy(T["off%d" % s][:, 0:8], T.bn[:, s:16:2]).then_inc(S["on%d" % s], 1)

    def stat(s, h, sem, n):
        v.wait_ge(S[sem], n)
        src = T.wx if h == 0 else T.wy
        v.quantize_mx(T["s%d%dq" % (s, h)][:, 0:512], T["s%d%ds" % (s, h)][:, 0:512], src[:, 0:2048]).then_inc(S["q%d%d" % (s, h)], 1)

    def wait_lists(queue, qs):
        for q in qs:
            if q == r:
                queue.wait_ge(S["on%d" % Q], 1)
            else:
                queue.wait_ge(S["a%d" % q], n_in if q == partner else n_off)

    def gather(call, qs, t, sem, *more):
        q0, n = min(qs), len(qs)
        lists = own[:, 0:8] if qs[0] == r else T.arr[:, 8 * q0:8 * (q0 + n)]
        call(T.e[:, 512 * q0 + t:512 * (q0 + n):4], T.wn[:, 256 * t:256 * t + 256].indirect(lists), *more).then_inc(S["%s%d" % (sem, q0)], 1)

    def vgather(u):
        qs, ts = units[u]
        wait_lists(v, qs)
        for t in ts:
            gather(v.tensor_copy, qs, t, "gv")

    def pack(u):
        qs, ts = units[u]
        q0, n = min(qs), len(qs)
        v.wait_ge(S["gv%d" % q0], len(ts))
        v.wait_ge(S["gs%d" % q0], 4 - len(ts))
        a, b = 128 * q0, 128 * (q0 + n)
        cq, cs = (T.rq, T.rs) if q0 == r else (T.eq, T.es)
        v.quantize_mx(cq[:, a:b], cs[:, a:b], T.e[:, 4 * a:4 * b]).then_inc(S["eq%d" % q0], 1)

    v.wait_ge(S.zs, 1)
    stat(Q, 0, "wx", 64)
    V(v.memset(T.wy[0:64, 0:1024], 0.0))
    v.wait_ge(S.sp, 4)
    vgather(0)
    vgather(1)
    pack(0)
    vsync()
    stat(Q, 1, "wy", 48)
    pack(1)
    vgather(2)
    stat(F, 0, "fx", 16)
    pack(2)
    vgather(3)
    stat(F, 1, "fy", 16)
    pack(3)
    vgather(4)
    pack(4)
    vgather(5)
    pack(5)

    def finish(call, o, h, *more):
        i = 2 * o + h
        call(T.yo[:, 128 * i:128 * i + 128], T.ps[:, 512 * i:512 * i + 128], *more).then_inc(S["y%d" % o], 1)

    for o in range(4):
        v.wait_ge(S["f%d" % (2 * o + 1)], 1)
        finish(v.tensor_copy, o, 1)

    sc = g.scalar
    sc.wait_ge(S.zt, 1)
    sc.activation(T.wx[64:128, 0:512], T.zt[64:128, :], copy).then_inc(S.zs, 1)
    sc.wait_ge(S.st, 32)
    for t in range(4):
        sc.activation(T.wn[:, 256 * t:256 * t + 256], T.st[:, t:1024:4], copy).then_inc(S.sp, 1)
    sc.wait_ge(S.sp, 4)
    for qs, ts in units:
        wait_lists(sc, qs)
        for t in range(4):
            if t not in ts:
                gather(sc.activation, qs, t, "gs", copy)
    for o in range(4):
        sc.wait_ge(S["f%d" % (2 * o)], 1)
        finish(sc.activation, o, 0, copy)

    te = g.tensor
    order = [q for qs, _ in units for q in qs]
    for q in order:
        s = q // 4
        if q == order[0]:
            te.wait_ge(S["eq%d" % r], 1)
            te.wait_ge(S["q%d0" % Q], 1)
            te.wait_ge(S["q%d1" % Q], 1)
        else:
            if q == far2[0]:
                te.wait_ge(S["q%d0" % F], 1)
                te.wait_ge(S["q%d1" % F], 1)
            te.wait_ge(S["n%d" % q], arrivals(q))
        for i in range(8):
            o, h = i // 2, i % 2
            w = slice(128 * o, 128 * o + 128)
            c = te.matmul_mx(T.ps[:, 512 * i:512 * i + 128], T["s%d%dq" % (s, h)][:, w], T["s%d%ds" % (s, h)][:, w],
                             T.rq[:, 128 * q:128 * q + 128], T.rs[:, 128 * q:128 * q + 128], q == order[0], q == order[-1])
            if q == order[-1]:
                c.then_inc(S["f%d" % i], 1)

    for o in range(4):
        g.sync.wait_ge(S["y%d" % o], 2)
        g.sync.dma_start(T.y[:, 256 * o:256 * o + 256], T.yo[:, 256 * o:256 * o + 256]).then_inc(S.yd, 16)
    g.sync.wait_ge(S.yd, 64)
